import numpy as np, ml_dtypes
CORES = [0,1,2,3,8,9,10,11]
N = 8
T = 32
ROUTE = [[[6],[2],[3],[2],[3],[2],[1],[2],[4],[0],[7],[7],[1],[0],[2],[7],[7],[4],[7],[1],[4],[2],[5],[4],[1],[5],[0],[3],[5],[5],[1],[4]],[[1],[3],[2],[7],[4],[4],[4],[3],[1],[7],[2],[2],[5],[7],[3],[2],[7],[4],[3],[3],[1],[2],[4],[5],[3],[6],[3],[4],[6],[1],[7],[5]],[[5],[4],[2],[6],[5],[3],[5],[0],[0],[7],[5],[7],[7],[1],[0],[1],[5],[6],[6],[7],[6],[6],[3],[4],[4],[5],[4],[2],[5],[1],[0],[4]],[[0],[6],[6],[6],[4],[4],[7],[6],[5],[5],[0],[6],[0],[7],[7],[1],[2],[3],[2],[3],[7],[2],[2],[0],[1],[1],[0],[3],[0],[7],[0],[2]],[[5],[4],[1],[2],[1],[2],[1],[7],[4],[4],[7],[7],[6],[6],[2],[5],[1],[3],[2],[2],[2],[7],[5],[4],[3],[2],[3],[1],[4],[3],[4],[7]],[[1],[3],[3],[6],[7],[5],[7],[2],[0],[2],[2],[3],[3],[0],[3],[4],[4],[7],[3],[5],[4],[3],[4],[7],[4],[0],[3],[5],[4],[3],[5],[3]],[[6],[5],[1],[1],[5],[7],[7],[5],[7],[7],[6],[3],[0],[1],[2],[0],[4],[1],[5],[3],[3],[5],[2],[1],[3],[4],[5],[2],[4],[7],[4],[2]],[[4],[2],[6],[0],[1],[3],[7],[0],[3],[7],[7],[2],[3],[5],[1],[1],[5],[2],[3],[3],[5],[2],[6],[3],[4],[7],[6],[0],[7],[5],[4],[3]]]
ZW = 40
def setup_inputs(rng):
    return {"z": rng.standard_normal((N, 128, ZW), dtype=np.float32).astype(ml_dtypes.bfloat16)}
def reference(z):
    y = np.zeros((N, 128, T), np.float64)
    fill = [0] * N
    for r in range(N):
        for t in range(T):
            for e in ROUTE[r][t]:
                y[r][:, t] += z[e][:, fill[e]].astype(np.float64)
                fill[e] += 1
    return {"y": y.astype(z.dtype)}

@@ -1,0 +1,256 @@
+import concourse.bass as bass
+
+P = 128
+NR = 8
+ZW = 40
+TN = 32
+
+SCRATCH = {
+    "zs": ("sbuf", [P, ZW], "bfloat16"),
+    "stage": ("sbuf", [P, NR * ZW], "bfloat16"),
+    "ybuf": ("sbuf", [P, TN], "bfloat16"),
+}
+SEMAPHORES = ["loaded", "stored", "copied", "arrived", "sent",
+              "blk0", "blk1", "blk2", "blk3", "blk4", "blk5", "blk6", "blk7"]
+
+MAXW = 2
+RELAY_ROT = 0
+DIRECT_FIRST = False
+SELF_FIRST = False
+CAP0 = 1.0
+SIMPLE = False
+
+
+def pieces_of(route, maxw):
+    fill = [0] * len(route)
+    out = []
+    for r in range(len(route)):
+        for t in range(len(route[r])):
+            e = route[r][t][0]
+            k = fill[e]
+            fill[e] += 1
+            if out:
+                le, lk, lw, lr, lt = out[-1]
+                if le == e and lr == r and lt + lw == t and lw < maxw:
+                    out[-1] = (le, lk, lw + 1, lr, lt)
+                    continue
+            out.append((e, k, 1, r, t))
+    return out
+
+
+def pick_engines(load, allowed, q, rows, limit, hold=0):
+    def seen(j):
+        return load[j] + (hold if j < 8 else 0)
+
+    order = sorted(allowed, key=lambda j: (seen(j), j))
+    best = None
+    for per in (1, 2, 4, 8, 16):
+        if q * per > min(len(order), limit):
+            break
+        top = max(seen(j) for j in order[:q * per]) + rows // per
+        if best is None or top <= best[0]:
+            best = (top, per)
+    per = best[1]
+    masks = []
+    for i in range(q):
+        m = 0
+        for j in order[i * per:(i + 1) * per]:
+            m |= 1 << j
+            load[j] += rows // per
+        masks.append((m, per))
+    return masks
+
+
+def assign(pcs, cores, topo, allc):
+    def is_port(c):
+        return any(topo.chip(d) != topo.chip(c) and topo.may_write(c, d) for d in allc)
+
+    def kind(ch, rank, port):
+        return [c for c in allc if topo.chip(c) == ch and (c in cores) == rank and is_port(c) == port]
+
+    def rot(lst, i):
+        return [lst[(i + j) % len(lst)] for j in range(len(lst))] if lst else []
+
+    def prefs(p):
+        ce, cr = cores[p[0]], cores[p[3]]
+        near, far = topo.chip(ce), topo.chip(cr)
+        same = kind(near, True, is_port(ce))
+        i = same.index(ce)
+        if near != far and not is_port(ce):
+            return 0, rot(kind(near, False, True), i)[:1] + rot(kind(near, True, True), i + RELAY_ROT) \
+                + rot(kind(near, False, True), i)[1:]
+        if near != far:
+            lst = rot(kind(far, False, False), i)[:1]
+            lst = ([ce] + lst) if DIRECT_FIRST else (lst + [ce])
+            return 1, lst + rot(kind(far, False, False), i)[1:] + rot(kind(far, False, True), i)
+        hl = rot(kind(near, False, True), i) + rot(kind(near, False, False), i)
+        if ce == cr:
+            return 3, hl
+        return (-1 if SELF_FIRST else 2), [ce] + hl
+
+    pf = dict((p, prefs(p)) for p in pcs)
+    order = sorted(pcs, key=lambda p: (pf[p][0], p[0], p[1]))
+    cap = 100.0 if SIMPLE else CAP0
+    while True:
+        tot = dict((c, 0) for c in allc)
+        low = dict((c, 0) for c in allc)
+        where = {}
+        for p in order:
+            cr = cores[p[3]]
+            for s in pf[p][1]:
+                x = topo.chip(s) != topo.chip(cr)
+                if tot[s] + 1 <= 16 * cap and (not x or low[s] + 1 <= 8 * cap):
+                    tot[s] += 1
+                    low[s] += 1 if x else 0
+                    where[p] = s
+                    break
+            else:
+                break
+        if len(where) == len(pcs):
+            return where
+        cap += 0.0625
+
+
+def build_plan(tables, cores, topo):
+    route = tables["ROUTE"]
+    pcs = pieces_of(route, MAXW)
+    chips = sorted(set(topo.chip(c) for c in cores))
+    allc = [ch * 8 + i for ch in chips for i in range(8)]
+    where = assign(pcs, cores, topo, allc)
+    opened = set((p[0], where[p]) for p in pcs if where[p] != cores[p[0]])
+
+    prog = dict((c, []) for c in allc)
+    arrived = dict((c, 0) for c in allc)
+    sent = dict((c, 0) for c in allc)
+    copies = dict((c, 0) for c in allc)
+    load = dict((c, [0] * 16) for c in allc)
+    blk_in = dict((c, {}) for c in allc)
+
+    for e in range(len(cores)):
+        ce = cores[e]
+        prog[ce].append(("load",))
+        dsts = sorted(s for (x, s) in opened if x == e)
+        if not dsts:
+            continue
+        win = {}
+        for p in pcs:
+            s = where[p]
+            if p[0] == e and s != ce:
+                lo, hi = win.get(s, (ZW, 0))
+                win[s] = (min(lo, p[1]), max(hi, p[1] + p[2]))
+        width = max(hi - lo for lo, hi in win.values())
+        far = [s for s in dsts if topo.chip(s) != topo.chip(ce)]
+        near = [s for s in dsts if topo.chip(s) == topo.chip(ce)]
+        trs = []
+        if far:
+            for s, mk in zip(far, pick_engines(load[ce], range(8), len(far), P, 8)):
+                trs.append((s, mk))
+        if near:
+            for s, mk in zip(near, pick_engines(load[ce], range(8, 16) if far else range(16), len(near), P, 16)):
+                trs.append((s, mk))
+        call = []
+        for s, (m, per) in trs:
+            lo = min(win[s][0], ZW - width)
+            call.append((s, lo, width, m))
+            blk_in[s][e] = per
+            sent[ce] += per
+        prog[ce].append(("blocks", e, call))
+
+    for s in allc:
+        groups = {}
+        for p in pcs:
+            if where[p] != s:
+                continue
+            ce = cores[p[0]]
+            cls = 0 if ce == s else (1 if topo.chip(ce) == topo.chip(s) else 2)
+            groups.setdefault((cls, p[2]), []).append(p)
+        waited = set()
+        ahead = sum(1 for p in pcs if where[p] == s and topo.chip(cores[p[3]]) != topo.chip(s))
+        for key in sorted(groups):
+            grp = groups[key]
+            for e in sorted(set(p[0] for p in grp)):
+                if cores[e] != s and e not in waited:
+                    waited.add(e)
+                    prog[s].append(("wait_blk", e, blk_in[s][e]))
+            calls = []
+            xs = [p for p in grp if topo.chip(cores[p[3]]) != topo.chip(s)]
+            ons = [p for p in grp if topo.chip(cores[p[3]]) == topo.chip(s) and cores[p[3]] != s]
+            while xs or ons:
+                qx = min(len(xs), 8)
+                qo = min(len(ons), 16 - qx)
+                call = []
+                used = 0
+                if qx:
+                    for p, (m, per) in zip(xs[:qx], pick_engines(load[s], range(8), qx, P, 16 - qo)):
+                        call.append((p, m, per))
+                        used |= m
+                    ahead -= qx
+                if qo:
+                    free = [j for j in range(16) if not used >> j & 1]
+                    for p, (m, per) in zip(ons[:qo], pick_engines(load[s], free, qo, P, 16, ahead * P // 8)):
+                        call.append((p, m, per))
+                xs = xs[qx:]
+                ons = ons[qo:]
+                for p, m, per in call:
+                    arrived[cores[p[3]]] += per
+                    sent[s] += per
+                calls.append([(p, m) for p, m, per in call])
+            for call in calls:
+                prog[s].append(("scatter", call))
+            for p in grp:
+                if cores[p[3]] == s:
+                    prog[s].append(("copy", p))
+                    copies[s] += 1
+    return {"prog": prog, "arrived": arrived, "sent": sent, "copies": copies, "where": where, "load": load}
+
+
+def rank_program(g, core, T, topo):
+    plan = build_plan(T.tables, T.cores, topo)
+    if core not in plan["prog"]:
+        return
+    blk = [T.sem.blk0, T.sem.blk1, T.sem.blk2, T.sem.blk3, T.sem.blk4, T.sem.blk5, T.sem.blk6, T.sem.blk7]
+    rank = T.rank_of(core)
+
+    def dst_id(c):
+        rid, pid, se = topo.addr(c)
+        return bass.DstId(rid=rid, pnc=pid)
+
+    def source(p):
+        e, k, w, r, t = p
+        if T.cores[e] == core:
+            return T.zs[:, k:k + w]
+        return T.stage[:, e * ZW + k:e * ZW + k + w]
+
+    for op in plan["prog"][core]:
+        if op[0] == "load":
+            g.dma_start(T.zs[:], T.z[:]).then_inc(T.sem.loaded, 16)
+            g.wait_ge(T.sem.loaded, 16)
+        elif op[0] == "blocks":
+            e = op[1]
+            g.remote_dma_fused(
+                [bass.RemoteDMATransfer(dst_ids=[dst_id(s)], dma_engine_mask=m, remote_sem=blk[e],
+                                        src=T.zs[:, lo:lo + wd], dst=T.stage[:, e * ZW + lo:e * ZW + lo + wd])
+                 for (s, lo, wd, m) in op[2]],
+                local_sem=T.sem.sent)
+        elif op[0] == "wait_blk":
+            g.wait_ge(blk[op[1]], op[2])
+        elif op[0] == "scatter":
+            g.remote_dma_fused(
+                [bass.RemoteDMATransfer(dst_ids=[dst_id(T.cores[p[3]])], dma_engine_mask=m, remote_sem=T.sem.arrived,
+                                        src=source(p), dst=T.ybuf[:, p[4]:p[4] + p[2]])
+                 for (p, m) in op[1]],
+                local_sem=T.sem.sent)
+        elif op[0] == "copy":
+            p = op[1]
+            g.dma_start(T.ybuf[:, p[4]:p[4] + p[2]], source(p)).then_inc(T.sem.copied, 16)
+
+    if rank is not None:
+        if plan["arrived"][core]:
+            g.wait_ge(T.sem.arrived, plan["arrived"][core])
+        if plan["copies"][core]:
+            g.wait_ge(T.sem.copied, 16 * plan["copies"][core])
+        g.dma_start(T.y[:], T.ybuf[:]).then_inc(T.sem.stored, 16)
+    if plan["sent"][core]:
+        g.wait_ge(T.sem.sent, plan["sent"][core])
+    if rank is not None:
+        g.wait_ge(T.sem.stored, 16)

@@ -10,15 +10,10 @@ SCRATCH = {
     "stage": ("sbuf", [P, NR * ZW], "bfloat16"),
     "ybuf": ("sbuf", [P, TN], "bfloat16"),
 }
-SEMAPHORES = ["loaded", "stored", "copied", "arrived", "sent",
+SEMAPHORES = ["loaded", "stored", "arrived", "sent",
               "blk0", "blk1", "blk2", "blk3", "blk4", "blk5", "blk6", "blk7"]
 
 MAXW = 2
-RELAY_ROT = 0
-DIRECT_FIRST = False
-SELF_FIRST = False
-CAP0 = 1.0
-SIMPLE = False
 
 
 def pieces_of(route, maxw):
@@ -77,20 +72,19 @@ def assign(pcs, cores, topo, allc):
         same = kind(near, True, is_port(ce))
         i = same.index(ce)
         if near != far and not is_port(ce):
-            return 0, rot(kind(near, False, True), i)[:1] + rot(kind(near, True, True), i + RELAY_ROT) \
+            return 0, rot(kind(near, False, True), i)[:1] + rot(kind(near, True, True), i) \
                 + rot(kind(near, False, True), i)[1:]
         if near != far:
-            lst = rot(kind(far, False, False), i)[:1]
-            lst = ([ce] + lst) if DIRECT_FIRST else (lst + [ce])
-            return 1, lst + rot(kind(far, False, False), i)[1:] + rot(kind(far, False, True), i)
+            return 1, rot(kind(far, False, False), i)[:1] + [ce] + rot(kind(far, False, False), i)[1:] \
+                + rot(kind(far, False, True), i)
         hl = rot(kind(near, False, True), i) + rot(kind(near, False, False), i)
         if ce == cr:
             return 3, hl
-        return (-1 if SELF_FIRST else 2), [ce] + hl
+        return 2, [ce] + hl
 
     pf = dict((p, prefs(p)) for p in pcs)
     order = sorted(pcs, key=lambda p: (pf[p][0], p[0], p[1]))
-    cap = 100.0 if SIMPLE else CAP0
+    cap = 1.0
     while True:
         tot = dict((c, 0) for c in allc)
         low = dict((c, 0) for c in allc)
@@ -122,7 +116,6 @@ def build_plan(tables, cores, topo):
     prog = dict((c, []) for c in allc)
     arrived = dict((c, 0) for c in allc)
     sent = dict((c, 0) for c in allc)
-    copies = dict((c, 0) for c in allc)
     load = dict((c, [0] * 16) for c in allc)
     blk_in = dict((c, {}) for c in allc)
 
@@ -172,9 +165,8 @@ def build_plan(tables, cores, topo):
                 if cores[e] != s and e not in waited:
                     waited.add(e)
                     prog[s].append(("wait_blk", e, blk_in[s][e]))
-            calls = []
             xs = [p for p in grp if topo.chip(cores[p[3]]) != topo.chip(s)]
-            ons = [p for p in grp if topo.chip(cores[p[3]]) == topo.chip(s) and cores[p[3]] != s]
+            ons = [p for p in grp if topo.chip(cores[p[3]]) == topo.chip(s)]
             while xs or ons:
                 qx = min(len(xs), 8)
                 qo = min(len(ons), 16 - qx)
@@ -194,14 +186,8 @@ def build_plan(tables, cores, topo):
                 for p, m, per in call:
                     arrived[cores[p[3]]] += per
                     sent[s] += per
-                calls.append([(p, m) for p, m, per in call])
-            for call in calls:
-                prog[s].append(("scatter", call))
-            for p in grp:
-                if cores[p[3]] == s:
-                    prog[s].append(("copy", p))
-                    copies[s] += 1
-    return {"prog": prog, "arrived": arrived, "sent": sent, "copies": copies, "where": where, "load": load}
+                prog[s].append(("scatter", [(p, m) for p, m, per in call]))
+    return {"prog": prog, "arrived": arrived, "sent": sent, "where": where, "load": load}
 
 
 def rank_program(g, core, T, topo):
@@ -240,15 +226,9 @@ def rank_program(g, core, T, topo):
                                         src=source(p), dst=T.ybuf[:, p[4]:p[4] + p[2]])
                  for (p, m) in op[1]],
                 local_sem=T.sem.sent)
-        elif op[0] == "copy":
-            p = op[1]
-            g.dma_start(T.ybuf[:, p[4]:p[4] + p[2]], source(p)).then_inc(T.sem.copied, 16)
 
     if rank is not None:
-        if plan["arrived"][core]:
-            g.wait_ge(T.sem.arrived, plan["arrived"][core])
-        if plan["copies"][core]:
-            g.wait_ge(T.sem.copied, 16 * plan["copies"][core])
+        g.wait_ge(T.sem.arrived, plan["arrived"][core])
         g.dma_start(T.y[:], T.ybuf[:]).then_inc(T.sem.stored, 16)
     if plan["sent"][core]:
         g.wait_ge(T.sem.sent, plan["sent"][core])

import concourse.bass as bass

P = 128
NR = 8
ZW = 40
TN = 32

SCRATCH = {
    "zs": ("sbuf", [P, ZW], "bfloat16"),
    "stage": ("sbuf", [P, NR * ZW], "bfloat16"),
    "ybuf": ("sbuf", [P, TN], "bfloat16"),
}
SEMAPHORES = ["loaded", "stored", "arrived", "sent",
              "blk0", "blk1", "blk2", "blk3", "blk4", "blk5", "blk6", "blk7"]

MAXW = 2


def pieces_of(route, maxw):
    fill = [0] * len(route)
    out = []
    for r in range(len(route)):
        for t in range(len(route[r])):
            e = route[r][t][0]
            k = fill[e]
            fill[e] += 1
            if out:
                le, lk, lw, lr, lt = out[-1]
                if le == e and lr == r and lt + lw == t and lw < maxw:
                    out[-1] = (le, lk, lw + 1, lr, lt)
                    continue
            out.append((e, k, 1, r, t))
    return out


def pick_engines(load, allowed, q, rows, limit, hold=0):
    def seen(j):
        return load[j] + (hold if j < 8 else 0)

    order = sorted(allowed, key=lambda j: (seen(j), j))
    best = None
    for per in (1, 2, 4, 8, 16):
        if q * per > min(len(order), limit):
            break
        top = max(seen(j) for j in order[:q * per]) + rows // per
        if best is None or top <= best[0]:
            best = (top, per)
    per = best[1]
    masks = []
    for i in range(q):
        m = 0
        for j in order[i * per:(i + 1) * per]:
            m |= 1 << j
            load[j] += rows // per
        masks.append((m, per))
    return masks


def assign(pcs, cores, topo, allc):
    def is_port(c):
        return any(topo.chip(d) != topo.chip(c) and topo.may_write(c, d) for d in allc)

    def kind(ch, rank, port):
        return [c for c in allc if topo.chip(c) == ch and (c in cores) == rank and is_port(c) == port]

    def rot(lst, i):
        return [lst[(i + j) % len(lst)] for j in range(len(lst))] if lst else []

    def prefs(p):
        ce, cr = cores[p[0]], cores[p[3]]
        near, far = topo.chip(ce), topo.chip(cr)
        same = kind(near, True, is_port(ce))
        i = same.index(ce)
        if near != far and not is_port(ce):
            return 0, rot(kind(near, False, True), i)[:1] + rot(kind(near, True, True), i) \
                + rot(kind(near, False, True), i)[1:]
        if near != far:
            return 1, rot(kind(far, False, False), i)[:1] + [ce] + rot(kind(far, False, False), i)[1:] \
                + rot(kind(far, False, True), i)
        hl = rot(kind(near, False, True), i) + rot(kind(near, False, False), i)
        if ce == cr:
            return 3, hl
        return 2, [ce] + hl

    pf = dict((p, prefs(p)) for p in pcs)
    order = sorted(pcs, key=lambda p: (pf[p][0], p[0], p[1]))
    cap = 1.0
    while True:
        tot = dict((c, 0) for c in allc)
        low = dict((c, 0) for c in allc)
        where = {}
        for p in order:
            cr = cores[p[3]]
            for s in pf[p][1]:
                x = topo.chip(s) != topo.chip(cr)
                if tot[s] + 1 <= 16 * cap and (not x or low[s] + 1 <= 8 * cap):
                    tot[s] += 1
                    low[s] += 1 if x else 0
                    where[p] = s
                    break
            else:
                break
        if len(where) == len(pcs):
            return where
        cap += 0.0625


def build_plan(tables, cores, topo):
    route = tables["ROUTE"]
    pcs = pieces_of(route, MAXW)
    chips = sorted(set(topo.chip(c) for c in cores))
    allc = [ch * 8 + i for ch in chips for i in range(8)]
    where = assign(pcs, cores, topo, allc)
    opened = set((p[0], where[p]) for p in pcs if where[p] != cores[p[0]])

    prog = dict((c, []) for c in allc)
    arrived = dict((c, 0) for c in allc)
    sent = dict((c, 0) for c in allc)
    load = dict((c, [0] * 16) for c in allc)
    blk_in = dict((c, {}) for c in allc)

    for e in range(len(cores)):
        ce = cores[e]
        prog[ce].append(("load",))
        dsts = sorted(s for (x, s) in opened if x == e)
        if not dsts:
            continue
        win = {}
        for p in pcs:
            s = where[p]
            if p[0] == e and s != ce:
                lo, hi = win.get(s, (ZW, 0))
                win[s] = (min(lo, p[1]), max(hi, p[1] + p[2]))
        width = max(hi - lo for lo, hi in win.values())
        far = [s for s in dsts if topo.chip(s) != topo.chip(ce)]
        near = [s for s in dsts if topo.chip(s) == topo.chip(ce)]
        trs = []
        if far:
            for s, mk in zip(far, pick_engines(load[ce], range(8), len(far), P, 8)):
                trs.append((s, mk))
        if near:
            for s, mk in zip(near, pick_engines(load[ce], range(8, 16) if far else range(16), len(near), P, 16)):
                trs.append((s, mk))
        call = []
        for s, (m, per) in trs:
            lo = min(win[s][0], ZW - width)
            call.append((s, lo, width, m))
            blk_in[s][e] = per
            sent[ce] += per
        prog[ce].append(("blocks", e, call))

    for s in allc:
        groups = {}
        for p in pcs:
            if where[p] != s:
                continue
            ce = cores[p[0]]
            cls = 0 if ce == s else (1 if topo.chip(ce) == topo.chip(s) else 2)
            groups.setdefault((cls, p[2]), []).append(p)
        waited = set()
        ahead = sum(1 for p in pcs if where[p] == s and topo.chip(cores[p[3]]) != topo.chip(s))
        for key in sorted(groups):
            grp = groups[key]
            for e in sorted(set(p[0] for p in grp)):
                if cores[e] != s and e not in waited:
                    waited.add(e)
                    prog[s].append(("wait_blk", e, blk_in[s][e]))
            xs = [p for p in grp if topo.chip(cores[p[3]]) != topo.chip(s)]
            ons = [p for p in grp if topo.chip(cores[p[3]]) == topo.chip(s)]
            while xs or ons:
                qx = min(len(xs), 8)
                qo = min(len(ons), 16 - qx)
                call = []
                used = 0
                if qx:
                    for p, (m, per) in zip(xs[:qx], pick_engines(load[s], range(8), qx, P, 16 - qo)):
                        call.append((p, m, per))
                        used |= m
                    ahead -= qx
                if qo:
                    free = [j for j in range(16) if not used >> j & 1]
                    for p, (m, per) in zip(ons[:qo], pick_engines(load[s], free, qo, P, 16, ahead * P // 8)):
                        call.append((p, m, per))
                xs = xs[qx:]
                ons = ons[qo:]
                for p, m, per in call:
                    arrived[cores[p[3]]] += per
                    sent[s] += per
                prog[s].append(("scatter", [(p, m) for p, m, per in call]))
    return {"prog": prog, "arrived": arrived, "sent": sent, "where": where, "load": load}


def rank_program(g, core, T, topo):
    plan = build_plan(T.tables, T.cores, topo)
    if core not in plan["prog"]:
        return
    blk = [T.sem.blk0, T.sem.blk1, T.sem.blk2, T.sem.blk3, T.sem.blk4, T.sem.blk5, T.sem.blk6, T.sem.blk7]
    rank = T.rank_of(core)

    def dst_id(c):
        rid, pid, se = topo.addr(c)
        return bass.DstId(rid=rid, pnc=pid)

    def source(p):
        e, k, w, r, t = p
        if T.cores[e] == core:
            return T.zs[:, k:k + w]
        return T.stage[:, e * ZW + k:e * ZW + k + w]

    for op in plan["prog"][core]:
        if op[0] == "load":
            g.dma_start(T.zs[:], T.z[:]).then_inc(T.sem.loaded, 16)
            g.wait_ge(T.sem.loaded, 16)
        elif op[0] == "blocks":
            e = op[1]
            g.remote_dma_fused(
                [bass.RemoteDMATransfer(dst_ids=[dst_id(s)], dma_engine_mask=m, remote_sem=blk[e],
                                        src=T.zs[:, lo:lo + wd], dst=T.stage[:, e * ZW + lo:e * ZW + lo + wd])
                 for (s, lo, wd, m) in op[2]],
                local_sem=T.sem.sent)
        elif op[0] == "wait_blk":
            g.wait_ge(blk[op[1]], op[2])
        elif op[0] == "scatter":
            g.remote_dma_fused(
                [bass.RemoteDMATransfer(dst_ids=[dst_id(T.cores[p[3]])], dma_engine_mask=m, remote_sem=T.sem.arrived,
                                        src=source(p), dst=T.ybuf[:, p[4]:p[4] + p[2]])
                 for (p, m) in op[1]],
                local_sem=T.sem.sent)

    if rank is not None:
        g.wait_ge(T.sem.arrived, plan["arrived"][core])
        g.dma_start(T.y[:], T.ybuf[:]).then_inc(T.sem.stored, 16)
    if plan["sent"][core]:
        g.wait_ge(T.sem.sent, plan["sent"][core])
    if rank is not None:
        g.wait_ge(T.sem.stored, 16)
